import numpy as np
import ml_dtypes


def mxq(x, axis, fmt="e4m3"):
    dtype, down = {"e4m3": (ml_dtypes.float8_e4m3fn, 7), "e5m2": (ml_dtypes.float8_e5m2, 14)}[fmt]
    v = np.moveaxis(np.asarray(x, np.float32).astype(ml_dtypes.bfloat16).astype(np.float64), axis, -1)
    blocks = v.reshape(v.shape[:-1] + (-1, 32))
    amax = np.abs(blocks).max(-1, keepdims=True)
    byte = np.maximum(np.where(amax > 0, np.frexp(amax)[1] - 1 + 127, 0) - down, 1)
    scale = np.exp2(byte - 127.0)
    codes = (blocks / scale).astype(np.float32).astype(dtype).astype(np.float64)
    return np.moveaxis((codes * scale).reshape(v.shape), -1, axis)


WIDE = False


def mx_kscale(k):
    if not WIDE:
        return np.ones(k)
    levels = np.array([10, -10, 5, -5, 0])
    if k % 512:
        return np.exp2(np.random.permutation(np.resize(levels, k // 32))).repeat(32)
    a = np.empty((k // 512, 16))
    for p in range(k // 512):
        a[p, :8] = np.random.permutation(np.resize(levels, 8))
        for g in range(8):
            far = levels[np.abs(levels - a[p, g]) >= 10]
            a[p, g + 8] = far[np.random.randint(len(far))]
    return np.exp2(a.ravel()).repeat(32)


def f64(x):
    return np.asarray(x).astype(np.float64)


def striped(idx):
    return np.tile(np.asarray(idx).reshape(-1, 16).T, (8, 1)).astype(np.uint16)


def unstriped(offs):
    return offs[:16].T.reshape(-1).astype(np.int64)


E2M1 = np.array([0.0, 0.5, 1.0, 1.5, 2.0, 3.0, 4.0, 6.0, -0.0, -0.5, -1.0, -1.5, -2.0, -3.0, -4.0, -6.0])


def pack_weight(w, fmt):
    k, n = w.shape
    w = f64(np.asarray(w, np.float32).astype(ml_dtypes.bfloat16)).reshape(k // 32, 32, n)
    amax = np.abs(w).max(1)
    if fmt == "e4m3":
        byte = np.frexp(amax)[1] - 1 + 127 - 7
    else:
        mant, ex = np.frexp(amax / 6.0)
        byte = np.where(mant > 0.5, ex, ex - 1) + 127
    byte = np.clip(np.where(amax > 0, byte, 1), 1, 254)
    scaled = (w * np.exp2(127.0 - byte)[:, None, :]).reshape(k, n).astype(np.float32)
    by_word = np.ascontiguousarray(scaled.reshape(k // 512, 128, 4, n).transpose(0, 1, 3, 2))
    if fmt == "e4m3":
        words = by_word.astype(ml_dtypes.float8_e4m3fn).view(np.uint8)
    else:
        c = by_word.astype(ml_dtypes.float4_e2m1fn).view(np.uint8) & 0xF
        words = (c[..., 0::2] | (c[..., 1::2] << 4)).reshape(k // 512, 128, 2 * n)
    return np.ascontiguousarray(words), np.ascontiguousarray(byte.astype(np.uint8).reshape(k // 512, 16, n))


def unpack_weight(words, scales, fmt):
    g, _, n = scales.shape
    words = np.ascontiguousarray(words).reshape(g, 128, n, -1)
    if fmt == "e4m3":
        vals = words.view(ml_dtypes.float8_e4m3fn).astype(np.float64)
    else:
        nib = np.empty((g, 128, n, 4), np.uint8)
        nib[..., 0::2] = words & 0xF
        nib[..., 1::2] = words >> 4
        vals = E2M1[nib]
    vals = vals * np.repeat(np.exp2(scales.astype(np.float64) - 127.0), 8, axis=1)[..., None]
    return vals.transpose(0, 1, 3, 2).reshape(g * 512, n)


D, E, T, I, Q, G, U = 512, 512, 2048, 512, 128, 64, 256


def setup_inputs():
    n = np.random.standard_normal
    idx = np.random.permutation(T)[:I]
    idx2 = np.random.permutation(U)[:G]
    fd = mx_kscale(D)
    fe = mx_kscale(E)
    keysp = pack_weight(n((D, T)) / fd[:, None], "e2m1")
    valsp = pack_weight(n((E, T)) / fe[:, None], "e2m1")
    return {
        "query": (n((D, Q)) * 0.6 / np.sqrt(D) * fd[:, None]).astype(np.float32),
        "keys_words": keysp[0],
        "keys_scales": keysp[1],
        "gout": (n((E, Q)) * 1 / np.sqrt(E) * fe[:, None]).astype(np.float32),
        "vals_words": valsp[0],
        "vals_scales": valsp[1],
        "pofs": (n((E, U)) / fe[:, None]).astype(np.float32),
        "pf": (np.random.uniform(0.5, 2.0, (Q, 1))).astype(np.float32),
        "dquery": (n((D, Q)) * 1.0 / np.sqrt(D) * fd[:, None]).astype(np.float32),
        "base": (0.5 * n((Q, I))).astype(np.float32),
        "offs": striped(idx),
        "offs2": striped(idx2),
    }


def reference(query, keys_words, keys_scales, gout, vals_words, vals_scales, pofs, pf, dquery, base, offs, offs2):
    idx = unstriped(offs)
    idx2 = unstriped(offs2)
    keysu = unpack_weight(keys_words, keys_scales, "e2m1")
    valsu = unpack_weight(vals_words, vals_scales, "e2m1")
    queryq = mxq(f64(query), 0, "e4m3")
    keysidxg = keysu[:, idx]
    a = queryq.T @ keysidxg
    dqueryq = mxq(f64(dquery), 0, "e4m3")
    ta = dqueryq.T @ keysidxg
    p = np.exp(a - np.max(a, axis=1, keepdims=True))
    z = np.sum(p, axis=1, keepdims=True)
    s = p.reshape(Q, G, I // G).sum(axis=2) * f64(pf)
    goutq = mxq(f64(gout), 0, "e4m3")
    valsidxg = valsu[:, idx]
    c0 = goutq.T @ valsidxg
    pofsidx2q = mxq(f64(pofs)[:, idx2], 0, "e4m3")
    c1 = goutq.T @ pofsidx2q
    ds = 1.0 / z * c1
    e1 = ds * f64(pf)
    r1 = np.repeat(e1, I // G, axis=1)
    dz = (np.sum(p * c0, axis=1, keepdims=True) + np.sum(s * c1, axis=1, keepdims=True)) / np.square(z) * (-1.0)
    dp = 1.0 / z * c0 + r1 + dz
    xp = ta * p
    xz = np.sum(xp, axis=1, keepdims=True)
    xs = xp.reshape(Q, G, I // G).sum(axis=2) * f64(pf)
    xds = xz * 1.0 / np.square(z) * (-1.0) * c1
    xe1 = xds * f64(pf)
    xr1 = np.repeat(xe1, I // G, axis=1)
    xdz = (np.sum(xp * c0, axis=1, keepdims=True) + np.sum(xs * c1, axis=1, keepdims=True) - xz * z * 2.0 * (np.sum(p * c0, axis=1, keepdims=True) + np.sum(s * c1, axis=1, keepdims=True)) / np.square(z)) / np.square(z) * (-1.0)
    xdp = xz * 1.0 / np.square(z) * (-1.0) * c0 + xr1 + xdz
    xda = xdp * p + xp * dp
    y = xda * 512.0 + f64(base)
    return y

@@ -1,0 +1,200 @@
+from contextlib import ExitStack
+
+import concourse.mybir as mybir
+
+D, E, T, I, Q, G, U = 512, 512, 2048, 512, 128, 64, 256
+FLOPS = 2 * Q * (2 * D * I + E * I + E * G)
+
+F32 = mybir.dt.float32
+BF16 = mybir.dt.bfloat16
+I32 = mybir.dt.int32
+U32 = mybir.dt.uint32
+U16 = mybir.dt.uint16
+U8 = mybir.dt.uint8
+FP8X4 = mybir.dt.float8_e4m3fn_x4
+FP4X4 = mybir.dt.float4_e2m1fn_x4
+ALU = mybir.AluOpType
+ACT = mybir.ActivationFunctionType
+
+P = 128
+PACK = 4
+PAGE = I // G
+GAIN = 512.0
+
+
+def load_scale_rows(queue, tile, scales):
+    for quad in range(4):
+        queue.dma_start(
+            out=tile[32 * quad : 32 * quad + 4, :].bitcast(I32),
+            in_=scales[0, 4 * quad : 4 * quad + 4, :].bitcast(I32),
+        )
+
+
+def interleave(nc, grouped, raw):
+    nc.scalar.copy(
+        out=grouped.rearrange("p (c i) t -> p c t i", i=4),
+        in_=raw.rearrange("p t (c i) -> p c t i", i=4),
+    )
+
+
+def tile_attend_hvpageoffsets_kernel(
+    tc, query, keys_words, keys_scales, gout, vals_words, vals_scales, pofs, pf, dquery, base, offs, offs2, out
+):
+    nc = tc.nc
+    with ExitStack() as ctx:
+        lists = ctx.enter_context(tc.tile_pool(name="lists", bufs=1))
+        sb = ctx.enter_context(tc.tile_pool(name="sb", bufs=1))
+        ps = ctx.enter_context(tc.psum_pool(name="ps", bufs=1))
+
+        slots = lists.tile([P, I // 16], U16, name="slots")
+        pages = lists.tile([P, G // 16], U16, name="pages")
+
+        k_words = sb.tile([P, T], U16, name="k_words", align_bytes=64)
+        k_scales = sb.tile([P, T], U8, name="k_scales", align_bytes=64)
+        v_words = sb.tile([P, T], U16, name="v_words", tag="v_words", align_bytes=64)
+        v_scales = sb.tile([P, T], U8, name="v_scales", tag="v_scales", align_bytes=64)
+        q_raw = sb.tile([P, PACK, Q], F32, name="q_raw", align_bytes=64)
+        dq_raw = sb.tile([P, PACK, Q], F32, name="dq_raw", align_bytes=64)
+        g_raw = sb.tile([P, PACK, Q], F32, name="g_raw", tag="g_raw", align_bytes=64)
+        po_raw = sb.tile([P, PACK * U], F32, name="po_raw", align_bytes=64)
+        base_sb = sb.tile([P, I], F32, name="base_sb", align_bytes=64)
+        pf_sb = sb.tile([P, 1], F32, name="pf_sb", align_bytes=64)
+        po_bf = sb.tile([P, (PACK + 1) * U], BF16, name="po_bf", tag="po_bf", align_bytes=64)
+
+        nc.vector.memset(k_scales[:, : T // 2].bitcast(I32), 0)
+        nc.gpsimd.memset(k_scales[:, T // 2 :].bitcast(I32), 0)
+        nc.vector.memset(v_scales[:, : T // 2].bitcast(I32), 0)
+        nc.gpsimd.memset(v_scales[:, T // 2 :].bitcast(I32), 0)
+        nc.gpsimd.memset(po_bf[:, PACK * U :], 0.0)
+        nc.sync.dma_start(slots[:], offs)
+        nc.sync.dma_start(pages[:], offs2)
+        nc.sync.dma_start(out=pf_sb[:], in_=pf)
+        nc.sync.dma_start(out=k_words[:].bitcast(I32), in_=keys_words[0].bitcast(I32))
+        nc.sync.dma_start(out=q_raw[:], in_=query.rearrange("(p j) w -> p j w", j=PACK))
+        load_scale_rows(nc.sync, k_scales, keys_scales)
+        nc.sync.dma_start(out=dq_raw[:], in_=dquery.rearrange("(p j) w -> p j w", j=PACK))
+        nc.sync.dma_start(out=po_raw[:], in_=pofs.rearrange("(p j) w -> p (j w)", j=PACK))
+        nc.sync.dma_start(out=v_words[:].bitcast(I32), in_=vals_words[0].bitcast(I32))
+        load_scale_rows(nc.sync, v_scales, vals_scales)
+        nc.sync.dma_start(out=g_raw[:], in_=gout.rearrange("(p j) w -> p j w", j=PACK))
+        nc.sync.dma_start(out=base_sb[:], in_=base)
+
+        def quantised(name, width, tag, codes_tag):
+            grouped = sb.tile([P, width, PACK], BF16, name=name + "_grouped", tag=tag, align_bytes=64)
+            codes = sb.tile([P, width], U32, name=name + "_codes", tag=codes_tag, align_bytes=64)
+            scales = sb.tile([P, width], U8, name=name + "_scales", align_bytes=64)
+            return grouped, codes, scales
+
+        def quantise(trio):
+            grouped, codes, scales = trio
+            nc.vector.quantize_mx(
+                out=codes[:].bitcast(FP8X4), scales=scales[:], in_=grouped[:].rearrange("p w t -> p (w t)")
+            )
+
+        def product(acc, rows, moving, moving_scales):
+            nc.tensor.matmul_mx(
+                out=acc[:],
+                lhsT=rows[1][:].bitcast(FP8X4),
+                lhsT_scale=rows[2][:],
+                rhs=moving,
+                rhs_scale=moving_scales,
+                start=True,
+                stop=True,
+            )
+
+        q_mx = quantised("q", Q, "q_grouped", "q_codes")
+        dq_mx = quantised("dq", Q, "dq_grouped", "dq_codes")
+        po_mx = quantised("po", G, "po_grouped", "v_words")
+
+        kw_g = sb.tile([P, I], U16, name="kw_g", align_bytes=64)
+        ks_g = sb.tile([P, I], U8, name="ks_g", align_bytes=64)
+        vw_g = sb.tile([P, I], U16, name="vw_g", align_bytes=64)
+        vs_g = sb.tile([P, I], U8, name="vs_g", align_bytes=64)
+
+        a = ps.tile([P, I], F32, name="a")
+        ta = ps.tile([P, I], F32, name="ta")
+        c0 = ps.tile([P, I], F32, name="c0")
+        c1 = ps.tile([P, G], F32, name="c1")
+
+        def column(name):
+            return sb.tile([P, 1], F32, name=name, align_bytes=64)
+
+        def row_tile(name):
+            return sb.tile([P, I], F32, name=name, align_bytes=64)
+
+        interleave(nc, q_mx[0][:], q_raw[:])
+        interleave(nc, dq_mx[0][:], dq_raw[:])
+        nc.vector.tensor_copy(ks_g[:], k_scales[:].indirect(slots[:]))
+        quantise(q_mx)
+        nc.vector.tensor_copy(kw_g[:], k_words[:].indirect(slots[:]))
+        product(a, q_mx, kw_g[:].bitcast(FP4X4), ks_g[:])
+        quantise(dq_mx)
+        product(ta, dq_mx, kw_g[:].bitcast(FP4X4), ks_g[:])
+
+        nc.scalar.activation(out=po_bf[:, : PACK * U], in_=po_raw[:], func=ACT.Copy)
+        for t in range(PACK):
+            nc.scalar.activation(
+                out=po_mx[0][:, :, t], in_=po_bf[:, t * U : (t + 2) * U].indirect(pages[:]), func=ACT.Copy
+            )
+        neg_max = sb.tile([P, 1], F32, name="neg_max", tag="after_exp", align_bytes=64)
+        nc.vector.tensor_reduce(out=neg_max[:], in_=a[:], axis=mybir.AxisListType.X, op=ALU.max, negate=True)
+        p = sb.tile([P, I], F32, name="p", tag="po_bf", align_bytes=64)
+        z = column("z")
+        nc.scalar.activation(out=p[:], in_=a[:], func=ACT.Exp, bias=neg_max[:], accum_out=z[:])
+
+        g_mx = quantised("g", Q, "after_exp", "v_scales")
+        interleave(nc, g_mx[0][:], g_raw[:])
+        nc.vector.tensor_copy(vw_g[:], v_words[:].indirect(slots[:]))
+        nc.vector.tensor_copy(vs_g[:], v_scales[:].indirect(slots[:]))
+        quantise(po_mx)
+        quantise(g_mx)
+        product(c0, g_mx, vw_g[:].bitcast(FP4X4), vs_g[:])
+        product(c1, g_mx, po_mx[1][:].bitcast(FP8X4), po_mx[2][:])
+
+        rz = sb.tile([P, 1], F32, name="rz", tag="after_exp", align_bytes=64)
+        nc.vector.reciprocal(out=rz[:], in_=z[:])
+        pn = sb.tile([P, I], F32, name="pn", tag="g_raw", align_bytes=64)
+        nc.scalar.activation(out=pn[:], in_=p[:], func=ACT.Copy, scale=rz[:])
+        neg_pf = column("neg_pf")
+        nc.gpsimd.tensor_scalar(out=neg_pf[:], in0=pf_sb[:], scalar1=-GAIN, scalar2=0.0, op0=ALU.mult, op1=ALU.add)
+        page_term = sb.tile([P, G], F32, name="page_term", align_bytes=64)
+        nc.scalar.activation(out=page_term[:], in_=c1[:], func=ACT.Copy, scale=neg_pf[:])
+
+        halves = [slice(0, I // 2), slice(I // 2, I)]
+        cn = row_tile("cn")
+        nc.vector.scalar_tensor_tensor(
+            out=cn[:].rearrange("p (g j) -> p g j", j=PAGE),
+            in0=c0[:].rearrange("p (g j) -> p g j", j=PAGE),
+            scalar=-GAIN,
+            in1=page_term[:].unsqueeze(2).to_broadcast([P, G, PAGE]),
+            op0=ALU.mult,
+            op1=ALU.add,
+        )
+        scratch = row_tile("scratch")
+        mean_ta = column("mean_ta")
+        nc.vector.scalar_tensor_tensor(
+            out=scratch[:], in0=ta[:], scalar=rz[:], in1=p[:], op0=ALU.mult, op1=ALU.mult, accum_out=mean_ta[:]
+        )
+        mean_cn = column("mean_cn")
+        scratch2 = row_tile("scratch2")
+        nc.vector.scalar_tensor_tensor(
+            out=scratch2[:], in0=cn[:], scalar=rz[:], in1=p[:], op0=ALU.mult, op1=ALU.mult, accum_out=mean_cn[:]
+        )
+        w = row_tile("w")
+        nc.vector.scalar_tensor_tensor(
+            out=w[:], in0=ta[:], scalar=mean_ta[:], in1=pn[:], op0=ALU.subtract, op1=ALU.mult
+        )
+        yn = row_tile("yn")
+        neg_cov = column("neg_cov")
+        nc.vector.scalar_tensor_tensor(
+            out=yn[:], in0=cn[:], scalar=mean_cn[:], in1=w[:], op0=ALU.subtract, op1=ALU.mult, accum_out=neg_cov[:]
+        )
+        y1 = row_tile("y1")
+        res = row_tile("res")
+        for h in halves:
+            nc.vector.tensor_tensor(out=y1[:, h], in0=base_sb[:, h], in1=yn[:, h], op=ALU.subtract)
+        for h in halves:
+            nc.vector.scalar_tensor_tensor(
+                out=res[:, h], in0=pn[:, h], scalar=neg_cov[:], in1=y1[:, h], op0=ALU.mult, op1=ALU.add
+            )
+            nc.sync.dma_start(out=out[:, h], in_=res[:, h])

@@ -44,28 +44,29 @@ def tile_attend_hvpageoffsets_kernel(
     with ExitStack() as ctx:
         lists = ctx.enter_context(tc.tile_pool(name="lists", bufs=1))
         sb = ctx.enter_context(tc.tile_pool(name="sb", bufs=1))
+        reuse = ctx.enter_context(tc.tile_pool(name="reuse", bufs=1))
         ps = ctx.enter_context(tc.psum_pool(name="ps", bufs=1))
 
         slots = lists.tile([P, I // 16], U16, name="slots")
         pages = lists.tile([P, G // 16], U16, name="pages")
 
         k_words = sb.tile([P, T], U16, name="k_words", align_bytes=64)
-        k_scales = sb.tile([P, T], U8, name="k_scales", align_bytes=64)
+        k_scales = sb.tile([P, T], U8, name="k_scales", tag="k_scales", align_bytes=64)
         v_words = sb.tile([P, T], U16, name="v_words", tag="v_words", align_bytes=64)
-        v_scales = sb.tile([P, T], U8, name="v_scales", tag="v_scales", align_bytes=64)
+        v_scales = reuse.tile([P, T], U8, name="v_scales", offset=0, align_bytes=64)
         q_raw = sb.tile([P, PACK, Q], F32, name="q_raw", align_bytes=64)
         dq_raw = sb.tile([P, PACK, Q], F32, name="dq_raw", align_bytes=64)
-        g_raw = sb.tile([P, PACK, Q], F32, name="g_raw", tag="g_raw", align_bytes=64)
-        po_raw = sb.tile([P, PACK * U], F32, name="po_raw", align_bytes=64)
+        g_raw = sb.tile([P, PACK, Q], F32, name="g_raw", align_bytes=64)
+        po_raw = sb.tile([P, PACK * U], F32, name="po_raw", tag="po_raw", align_bytes=64)
         base_sb = sb.tile([P, I], F32, name="base_sb", align_bytes=64)
         pf_sb = sb.tile([P, 1], F32, name="pf_sb", align_bytes=64)
-        po_bf = sb.tile([P, (PACK + 1) * U], BF16, name="po_bf", tag="po_bf", align_bytes=64)
+        po_bf = sb.tile([P, (PACK + 1) * U], BF16, name="po_bf", align_bytes=64)
 
         nc.vector.memset(k_scales[:, : T // 2].bitcast(I32), 0)
         nc.gpsimd.memset(k_scales[:, T // 2 :].bitcast(I32), 0)
         nc.vector.memset(v_scales[:, : T // 2].bitcast(I32), 0)
         nc.gpsimd.memset(v_scales[:, T // 2 :].bitcast(I32), 0)
-        nc.gpsimd.memset(po_bf[:, PACK * U :], 0.0)
+        nc.vector.memset(po_bf[:, PACK * U :], 0.0)
         nc.sync.dma_start(slots[:], offs)
         nc.sync.dma_start(pages[:], offs2)
         nc.sync.dma_start(out=pf_sb[:], in_=pf)
@@ -73,15 +74,15 @@ def tile_attend_hvpageoffsets_kernel(
         nc.sync.dma_start(out=q_raw[:], in_=query.rearrange("(p j) w -> p j w", j=PACK))
         load_scale_rows(nc.sync, k_scales, keys_scales)
         nc.sync.dma_start(out=dq_raw[:], in_=dquery.rearrange("(p j) w -> p j w", j=PACK))
+        load_scale_rows(nc.gpsimd, v_scales, vals_scales)
+        nc.sync.dma_start(out=g_raw[:], in_=gout.rearrange("(p j) w -> p j w", j=PACK))
         nc.sync.dma_start(out=po_raw[:], in_=pofs.rearrange("(p j) w -> p (j w)", j=PACK))
         nc.sync.dma_start(out=v_words[:].bitcast(I32), in_=vals_words[0].bitcast(I32))
-        load_scale_rows(nc.sync, v_scales, vals_scales)
-        nc.sync.dma_start(out=g_raw[:], in_=gout.rearrange("(p j) w -> p j w", j=PACK))
         nc.sync.dma_start(out=base_sb[:], in_=base)
 
-        def quantised(name, width, tag, codes_tag):
-            grouped = sb.tile([P, width, PACK], BF16, name=name + "_grouped", tag=tag, align_bytes=64)
-            codes = sb.tile([P, width], U32, name=name + "_codes", tag=codes_tag, align_bytes=64)
+        def quantised(name, grouped):
+            width = grouped.shape[1]
+            codes = sb.tile([P, width], U32, name=name + "_codes", align_bytes=64)
             scales = sb.tile([P, width], U8, name=name + "_scales", align_bytes=64)
             return grouped, codes, scales
 
@@ -102,14 +103,14 @@ def tile_attend_hvpageoffsets_kernel(
                 stop=True,
             )
 
-        q_mx = quantised("q", Q, "q_grouped", "q_codes")
-        dq_mx = quantised("dq", Q, "dq_grouped", "dq_codes")
-        po_mx = quantised("po", G, "po_grouped", "v_words")
+        q_mx = quantised("q", sb.tile([P, Q, PACK], BF16, name="q_grouped", align_bytes=64))
+        dq_mx = quantised("dq", sb.tile([P, Q, PACK], BF16, name="dq_grouped", align_bytes=64))
+        g_mx = quantised("g", sb.tile([P, Q, PACK], BF16, name="g_grouped", align_bytes=64))
 
         kw_g = sb.tile([P, I], U16, name="kw_g", align_bytes=64)
         ks_g = sb.tile([P, I], U8, name="ks_g", align_bytes=64)
-        vw_g = sb.tile([P, I], U16, name="vw_g", align_bytes=64)
-        vs_g = sb.tile([P, I], U8, name="vs_g", align_bytes=64)
+        vw_g = reuse.tile([P, I], U16, name="vw_g", offset=0, align_bytes=64)
+        vs_g = sb.tile([P, I], U8, name="vs_g", tag="k_scales", align_bytes=64)
 
         a = ps.tile([P, I], F32, name="a")
         ta = ps.tile([P, I], F32, name="ta")
@@ -124,77 +125,81 @@ def tile_attend_hvpageoffsets_kernel(
 
         interleave(nc, q_mx[0][:], q_raw[:])
         interleave(nc, dq_mx[0][:], dq_raw[:])
-        nc.vector.tensor_copy(ks_g[:], k_scales[:].indirect(slots[:]))
-        quantise(q_mx)
+        interleave(nc, g_mx[0][:], g_raw[:])
         nc.vector.tensor_copy(kw_g[:], k_words[:].indirect(slots[:]))
+        quantise(q_mx)
+        nc.vector.tensor_copy(ks_g[:], k_scales[:].indirect(slots[:]))
         product(a, q_mx, kw_g[:].bitcast(FP4X4), ks_g[:])
         quantise(dq_mx)
         product(ta, dq_mx, kw_g[:].bitcast(FP4X4), ks_g[:])
+        quantise(g_mx)
+        nc.vector.tensor_copy(vs_g[:], v_scales[:].indirect(slots[:]))
 
         nc.scalar.activation(out=po_bf[:, : PACK * U], in_=po_raw[:], func=ACT.Copy)
+        neg_max = reuse.tile([P, 1], F32, name="neg_max", offset=1024, align_bytes=64)
+        nc.vector.tensor_reduce(out=neg_max[:], in_=a[:], axis=mybir.AxisListType.X, op=ALU.max, negate=True)
+        p = sb.tile([P, I], F32, name="p", tag="po_raw", align_bytes=64)
+        z = column("z")
+        nc.scalar.activation(out=p[:], in_=a[:], func=ACT.Exp, bias=neg_max[:], accum_out=z[:])
+
+        po_mx = quantised("po", reuse.tile([P, G, PACK], BF16, name="po_grouped", offset=1024, align_bytes=64))
         for t in range(PACK):
             nc.scalar.activation(
                 out=po_mx[0][:, :, t], in_=po_bf[:, t * U : (t + 2) * U].indirect(pages[:]), func=ACT.Copy
             )
-        neg_max = sb.tile([P, 1], F32, name="neg_max", tag="after_exp", align_bytes=64)
-        nc.vector.tensor_reduce(out=neg_max[:], in_=a[:], axis=mybir.AxisListType.X, op=ALU.max, negate=True)
-        p = sb.tile([P, I], F32, name="p", tag="po_bf", align_bytes=64)
-        z = column("z")
-        nc.scalar.activation(out=p[:], in_=a[:], func=ACT.Exp, bias=neg_max[:], accum_out=z[:])
-
-        g_mx = quantised("g", Q, "after_exp", "v_scales")
-        interleave(nc, g_mx[0][:], g_raw[:])
         nc.vector.tensor_copy(vw_g[:], v_words[:].indirect(slots[:]))
-        nc.vector.tensor_copy(vs_g[:], v_scales[:].indirect(slots[:]))
-        quantise(po_mx)
-        quantise(g_mx)
         product(c0, g_mx, vw_g[:].bitcast(FP4X4), vs_g[:])
-        product(c1, g_mx, po_mx[1][:].bitcast(FP8X4), po_mx[2][:])
 
-        rz = sb.tile([P, 1], F32, name="rz", tag="after_exp", align_bytes=64)
+        rz = sb.tile([P, 1], F32, name="rz", tag="v_words", align_bytes=64)
         nc.vector.reciprocal(out=rz[:], in_=z[:])
-        pn = sb.tile([P, I], F32, name="pn", tag="g_raw", align_bytes=64)
-        nc.scalar.activation(out=pn[:], in_=p[:], func=ACT.Copy, scale=rz[:])
-        neg_pf = column("neg_pf")
-        nc.gpsimd.tensor_scalar(out=neg_pf[:], in0=pf_sb[:], scalar1=-GAIN, scalar2=0.0, op0=ALU.mult, op1=ALU.add)
-        page_term = sb.tile([P, G], F32, name="page_term", align_bytes=64)
-        nc.scalar.activation(out=page_term[:], in_=c1[:], func=ACT.Copy, scale=neg_pf[:])
-
-        halves = [slice(0, I // 2), slice(I // 2, I)]
-        cn = row_tile("cn")
-        nc.vector.scalar_tensor_tensor(
-            out=cn[:].rearrange("p (g j) -> p g j", j=PAGE),
-            in0=c0[:].rearrange("p (g j) -> p g j", j=PAGE),
-            scalar=-GAIN,
-            in1=page_term[:].unsqueeze(2).to_broadcast([P, G, PAGE]),
-            op0=ALU.mult,
-            op1=ALU.add,
-        )
         scratch = row_tile("scratch")
         mean_ta = column("mean_ta")
         nc.vector.scalar_tensor_tensor(
             out=scratch[:], in0=ta[:], scalar=rz[:], in1=p[:], op0=ALU.mult, op1=ALU.mult, accum_out=mean_ta[:]
         )
-        mean_cn = column("mean_cn")
+        quantise(po_mx)
+        product(c1, g_mx, po_mx[1][:].bitcast(FP8X4), po_mx[2][:])
+        gain_pf = column("gain_pf")
+        nc.gpsimd.tensor_scalar(out=gain_pf[:], in0=pf_sb[:], scalar1=GAIN, scalar2=0.0, op0=ALU.mult, op1=ALU.add)
+        neg_rz2 = column("neg_rz2")
+        nc.gpsimd.tensor_scalar(out=neg_rz2[:], in0=rz[:], scalar1=rz[:], scalar2=-1.0, op0=ALU.mult, op1=ALU.mult)
+        page_term = sb.tile([P, G], F32, name="page_term", align_bytes=64)
+        nc.scalar.activation(out=page_term[:], in_=c1[:], func=ACT.Copy, scale=gain_pf[:])
+
+        w = reuse.tile([P, I], F32, name="w", offset=1024, align_bytes=64)
+        nc.vector.scalar_tensor_tensor(
+            out=w[:], in0=ta[:], scalar=mean_ta[:], in1=p[:], op0=ALU.subtract, op1=ALU.mult
+        )
+        c = row_tile("c")
+        nc.vector.scalar_tensor_tensor(
+            out=c[:].rearrange("p (g j) -> p g j", j=PAGE),
+            in0=c0[:].rearrange("p (g j) -> p g j", j=PAGE),
+            scalar=GAIN,
+            in1=page_term[:].unsqueeze(2).to_broadcast([P, G, PAGE]),
+            op0=ALU.mult,
+            op1=ALU.add,
+        )
+        mean_c = column("mean_c")
         scratch2 = row_tile("scratch2")
         nc.vector.scalar_tensor_tensor(
-            out=scratch2[:], in0=cn[:], scalar=rz[:], in1=p[:], op0=ALU.mult, op1=ALU.mult, accum_out=mean_cn[:]
+            out=scratch2[:], in0=c[:], scalar=rz[:], in1=p[:], op0=ALU.mult, op1=ALU.mult, accum_out=mean_c[:]
         )
-        w = row_tile("w")
+        y = row_tile("y")
+        cov_z = column("cov_z")
         nc.vector.scalar_tensor_tensor(
-            out=w[:], in0=ta[:], scalar=mean_ta[:], in1=pn[:], op0=ALU.subtract, op1=ALU.mult
+            out=y[:], in0=c[:], scalar=mean_c[:], in1=w[:], op0=ALU.subtract, op1=ALU.mult, accum_out=cov_z[:]
         )
-        yn = row_tile("yn")
-        neg_cov = column("neg_cov")
-        nc.vector.scalar_tensor_tensor(
-            out=yn[:], in0=cn[:], scalar=mean_cn[:], in1=w[:], op0=ALU.subtract, op1=ALU.mult, accum_out=neg_cov[:]
-        )
+        p_factor = column("p_factor")
+        nc.scalar.activation(out=p_factor[:], in_=cov_z[:], func=ACT.Copy, scale=neg_rz2[:])
+        halves = [slice(0, I // 2), slice(I // 2, I)]
         y1 = row_tile("y1")
         res = row_tile("res")
         for h in halves:
-            nc.vector.tensor_tensor(out=y1[:, h], in0=base_sb[:, h], in1=yn[:, h], op=ALU.subtract)
+            nc.vector.scalar_tensor_tensor(
+                out=y1[:, h], in0=y[:, h], scalar=rz[:], in1=base_sb[:, h], op0=ALU.mult, op1=ALU.add
+            )
         for h in halves:
             nc.vector.scalar_tensor_tensor(
-                out=res[:, h], in0=pn[:, h], scalar=neg_cov[:], in1=y1[:, h], op0=ALU.mult, op1=ALU.add
+                out=res[:, h], in0=p[:, h], scalar=p_factor[:], in1=y1[:, h], op0=ALU.mult, op1=ALU.add
             )
             nc.sync.dma_start(out=out[:, h], in_=res[:, h])

@@ -30,8 +30,8 @@ def load_scale_rows(queue, tile, scales):
         )
 
 
-def interleave(nc, grouped, raw):
-    nc.scalar.copy(
+def interleave(copy, grouped, raw):
+    copy(
         out=grouped.rearrange("p (c i) t -> p c t i", i=4),
         in_=raw.rearrange("p t (c i) -> p c t i", i=4),
     )
@@ -44,7 +44,6 @@ def tile_attend_hvpageoffsets_kernel(
     with ExitStack() as ctx:
         lists = ctx.enter_context(tc.tile_pool(name="lists", bufs=1))
         sb = ctx.enter_context(tc.tile_pool(name="sb", bufs=1))
-        reuse = ctx.enter_context(tc.tile_pool(name="reuse", bufs=1))
         ps = ctx.enter_context(tc.psum_pool(name="ps", bufs=1))
 
         slots = lists.tile([P, I // 16], U16, name="slots")
@@ -53,14 +52,14 @@ def tile_attend_hvpageoffsets_kernel(
         k_words = sb.tile([P, T], U16, name="k_words", align_bytes=64)
         k_scales = sb.tile([P, T], U8, name="k_scales", tag="k_scales", align_bytes=64)
         v_words = sb.tile([P, T], U16, name="v_words", tag="v_words", align_bytes=64)
-        v_scales = reuse.tile([P, T], U8, name="v_scales", offset=0, align_bytes=64)
+        v_scales = sb.tile([P, T], U8, name="v_scales", tag="v_scales", align_bytes=64)
         q_raw = sb.tile([P, PACK, Q], F32, name="q_raw", align_bytes=64)
         dq_raw = sb.tile([P, PACK, Q], F32, name="dq_raw", align_bytes=64)
-        g_raw = sb.tile([P, PACK, Q], F32, name="g_raw", align_bytes=64)
-        po_raw = sb.tile([P, PACK * U], F32, name="po_raw", tag="po_raw", align_bytes=64)
+        g_raw = sb.tile([P, PACK, Q], F32, name="g_raw", tag="g_raw", align_bytes=64)
+        po_raw = sb.tile([P, PACK * U], F32, name="po_raw", align_bytes=64)
         base_sb = sb.tile([P, I], F32, name="base_sb", align_bytes=64)
         pf_sb = sb.tile([P, 1], F32, name="pf_sb", align_bytes=64)
-        po_bf = sb.tile([P, (PACK + 1) * U], BF16, name="po_bf", align_bytes=64)
+        po_bf = sb.tile([P, (PACK + 1) * U], BF16, name="po_bf", tag="po_bf", align_bytes=64)
 
         nc.vector.memset(k_scales[:, : T // 2].bitcast(I32), 0)
         nc.gpsimd.memset(k_scales[:, T // 2 :].bitcast(I32), 0)
@@ -74,43 +73,30 @@ def tile_attend_hvpageoffsets_kernel(
         nc.sync.dma_start(out=q_raw[:], in_=query.rearrange("(p j) w -> p j w", j=PACK))
         load_scale_rows(nc.sync, k_scales, keys_scales)
         nc.sync.dma_start(out=dq_raw[:], in_=dquery.rearrange("(p j) w -> p j w", j=PACK))
-        load_scale_rows(nc.gpsimd, v_scales, vals_scales)
-        nc.sync.dma_start(out=g_raw[:], in_=gout.rearrange("(p j) w -> p j w", j=PACK))
         nc.sync.dma_start(out=po_raw[:], in_=pofs.rearrange("(p j) w -> p (j w)", j=PACK))
         nc.sync.dma_start(out=v_words[:].bitcast(I32), in_=vals_words[0].bitcast(I32))
+        load_scale_rows(nc.sync, v_scales, vals_scales)
+        nc.sync.dma_start(out=g_raw[:], in_=gout.rearrange("(p j) w -> p j w", j=PACK))
         nc.sync.dma_start(out=base_sb[:], in_=base)
 
-        def quantised(name, grouped):
-            width = grouped.shape[1]
-            codes = sb.tile([P, width], U32, name=name + "_codes", align_bytes=64)
-            scales = sb.tile([P, width], U8, name=name + "_scales", align_bytes=64)
-            return grouped, codes, scales
+        def quantised():
+            return None
 
-        def quantise(trio):
-            grouped, codes, scales = trio
+        def quantise(codes, scales, grouped):
             nc.vector.quantize_mx(
-                out=codes[:].bitcast(FP8X4), scales=scales[:], in_=grouped[:].rearrange("p w t -> p (w t)")
+                out=codes.bitcast(FP8X4), scales=scales, in_=grouped.rearrange("p w t -> p (w t)")
             )
 
-        def product(acc, rows, moving, moving_scales):
+        def product(acc, row_codes, row_scales, moving, moving_scales):
             nc.tensor.matmul_mx(
                 out=acc[:],
-                lhsT=rows[1][:].bitcast(FP8X4),
-                lhsT_scale=rows[2][:],
+                lhsT=row_codes.bitcast(FP8X4),
+                lhsT_scale=row_scales,
                 rhs=moving,
                 rhs_scale=moving_scales,
                 start=True,
                 stop=True,
             )
-
-        q_mx = quantised("q", sb.tile([P, Q, PACK], BF16, name="q_grouped", align_bytes=64))
-        dq_mx = quantised("dq", sb.tile([P, Q, PACK], BF16, name="dq_grouped", align_bytes=64))
-        g_mx = quantised("g", sb.tile([P, Q, PACK], BF16, name="g_grouped", align_bytes=64))
-
-        kw_g = sb.tile([P, I], U16, name="kw_g", align_bytes=64)
-        ks_g = sb.tile([P, I], U8, name="ks_g", align_bytes=64)
-        vw_g = reuse.tile([P, I], U16, name="vw_g", offset=0, align_bytes=64)
-        vs_g = sb.tile([P, I], U8, name="vs_g", tag="k_scales", align_bytes=64)
 
         a = ps.tile([P, I], F32, name="a")
         ta = ps.tile([P, I], F32, name="ta")
@@ -123,53 +109,62 @@ def tile_attend_hvpageoffsets_kernel(
         def row_tile(name):
             return sb.tile([P, I], F32, name=name, align_bytes=64)
 
-        interleave(nc, q_mx[0][:], q_raw[:])
-        interleave(nc, dq_mx[0][:], dq_raw[:])
-        interleave(nc, g_mx[0][:], g_raw[:])
+        qd_grouped = sb.tile([P, 2 * Q, PACK], BF16, name="qd_grouped", tag="qd_grouped", align_bytes=64)
+        interleave(nc.scalar.copy, qd_grouped[:, :Q, :], q_raw[:])
+        interleave(nc.scalar.copy, qd_grouped[:, Q:, :], dq_raw[:])
+        kw_g = sb.tile([P, I], U16, name="kw_g", align_bytes=64)
         nc.vector.tensor_copy(kw_g[:], k_words[:].indirect(slots[:]))
-        quantise(q_mx)
+        ks_g = sb.tile([P, I], U8, name="ks_g", align_bytes=64)
         nc.vector.tensor_copy(ks_g[:], k_scales[:].indirect(slots[:]))
-        product(a, q_mx, kw_g[:].bitcast(FP4X4), ks_g[:])
-        quantise(dq_mx)
-        product(ta, dq_mx, kw_g[:].bitcast(FP4X4), ks_g[:])
-        quantise(g_mx)
+        qd_codes = sb.tile([P, 2 * Q], U32, name="qd_codes", tag="k_scales", align_bytes=64)
+        qd_scales = sb.tile([P, 2 * Q], U8, name="qd_scales", align_bytes=64)
+        quantise(qd_codes[:], qd_scales[:], qd_grouped[:])
+        product(a, qd_codes[:, :Q], qd_scales[:, :Q], kw_g[:].bitcast(FP4X4), ks_g[:])
+        product(ta, qd_codes[:, Q:], qd_scales[:, Q:], kw_g[:].bitcast(FP4X4), ks_g[:])
+        vw_g = sb.tile([P, I], U16, name="vw_g", tag="qd_grouped", align_bytes=64)
+        nc.vector.tensor_copy(vw_g[:], v_words[:].indirect(slots[:]))
+        neg_max = sb.tile([P, 1], F32, name="neg_max", tag="v_words", align_bytes=64)
+        neg_a = sb.tile([P, I], F32, name="neg_a", tag="neg_a", align_bytes=64)
+        nc.vector.tensor_scalar(
+            out=neg_a[:], in0=a[:], scalar1=-1.0, scalar2=None, op0=ALU.mult, op1=ALU.min, accum_out=neg_max[:]
+        )
+        vs_g = sb.tile([P, I], U8, name="vs_g", tag="neg_a", align_bytes=64)
         nc.vector.tensor_copy(vs_g[:], v_scales[:].indirect(slots[:]))
 
         nc.scalar.activation(out=po_bf[:, : PACK * U], in_=po_raw[:], func=ACT.Copy)
-        neg_max = reuse.tile([P, 1], F32, name="neg_max", offset=1024, align_bytes=64)
-        nc.vector.tensor_reduce(out=neg_max[:], in_=a[:], axis=mybir.AxisListType.X, op=ALU.max, negate=True)
-        p = sb.tile([P, I], F32, name="p", tag="po_raw", align_bytes=64)
-        z = column("z")
-        nc.scalar.activation(out=p[:], in_=a[:], func=ACT.Exp, bias=neg_max[:], accum_out=z[:])
-
-        po_mx = quantised("po", reuse.tile([P, G, PACK], BF16, name="po_grouped", offset=1024, align_bytes=64))
+        po_grouped = sb.tile([P, G, PACK], BF16, name="po_grouped", tag="po_grouped", align_bytes=64)
         for t in range(PACK):
             nc.scalar.activation(
-                out=po_mx[0][:, :, t], in_=po_bf[:, t * U : (t + 2) * U].indirect(pages[:]), func=ACT.Copy
+                out=po_grouped[:, :, t], in_=po_bf[:, t * U : (t + 2) * U].indirect(pages[:]), func=ACT.Copy
             )
-        nc.vector.tensor_copy(vw_g[:], v_words[:].indirect(slots[:]))
-        product(c0, g_mx, vw_g[:].bitcast(FP4X4), vs_g[:])
+        g_grouped = sb.tile([P, Q, PACK], BF16, name="g_grouped", tag="po_bf", align_bytes=64)
+        interleave(nc.scalar.copy, g_grouped[:], g_raw[:])
+        p = sb.tile([P, I], F32, name="p", tag="g_raw", align_bytes=64)
+        z = sb.tile([P, 1], F32, name="z", tag="z", align_bytes=64)
+        nc.scalar.activation(out=p[:], in_=a[:], func=ACT.Exp, bias=neg_max[:], accum_out=z[:])
 
-        rz = sb.tile([P, 1], F32, name="rz", tag="v_words", align_bytes=64)
+        rz = sb.tile([P, 1], F32, name="rz", tag="v_scales", align_bytes=64)
         nc.vector.reciprocal(out=rz[:], in_=z[:])
-        scratch = row_tile("scratch")
+        gp_codes = sb.tile([P, Q + G], U32, name="gp_codes", tag="z", align_bytes=64)
+        g_scales = sb.tile([P, Q], U8, name="g_scales", align_bytes=64)
+        po_scales = sb.tile([P, G], U8, name="po_scales", align_bytes=64)
+        quantise(gp_codes[:, :Q], g_scales[:], g_grouped[:])
+        product(c0, gp_codes[:, :Q], g_scales[:], vw_g[:].bitcast(FP4X4), vs_g[:])
+        quantise(gp_codes[:, Q:], po_scales[:], po_grouped[:])
+        product(c1, gp_codes[:, :Q], g_scales[:], gp_codes[:, Q:].bitcast(FP8X4), po_scales[:])
+
+        scratch = sb.tile([P, I], F32, name="scratch", tag="po_grouped", align_bytes=64)
         mean_ta = column("mean_ta")
         nc.vector.scalar_tensor_tensor(
             out=scratch[:], in0=ta[:], scalar=rz[:], in1=p[:], op0=ALU.mult, op1=ALU.mult, accum_out=mean_ta[:]
         )
-        quantise(po_mx)
-        product(c1, g_mx, po_mx[1][:].bitcast(FP8X4), po_mx[2][:])
         gain_pf = column("gain_pf")
         nc.gpsimd.tensor_scalar(out=gain_pf[:], in0=pf_sb[:], scalar1=GAIN, scalar2=0.0, op0=ALU.mult, op1=ALU.add)
         neg_rz2 = column("neg_rz2")
         nc.gpsimd.tensor_scalar(out=neg_rz2[:], in0=rz[:], scalar1=rz[:], scalar2=-1.0, op0=ALU.mult, op1=ALU.mult)
-        page_term = sb.tile([P, G], F32, name="page_term", align_bytes=64)
+        page_term = sb.tile([P, G], F32, name="page_term", tag="page_term", align_bytes=64)
         nc.scalar.activation(out=page_term[:], in_=c1[:], func=ACT.Copy, scale=gain_pf[:])
 
-        w = reuse.tile([P, I], F32, name="w", offset=1024, align_bytes=64)
-        nc.vector.scalar_tensor_tensor(
-            out=w[:], in0=ta[:], scalar=mean_ta[:], in1=p[:], op0=ALU.subtract, op1=ALU.mult
-        )
         c = row_tile("c")
         nc.vector.scalar_tensor_tensor(
             out=c[:].rearrange("p (g j) -> p g j", j=PAGE),
@@ -178,6 +173,10 @@ def tile_attend_hvpageoffsets_kernel(
             in1=page_term[:].unsqueeze(2).to_broadcast([P, G, PAGE]),
             op0=ALU.mult,
             op1=ALU.add,
+        )
+        w = sb.tile([P, I], F32, name="w", tag="page_term", align_bytes=64)
+        nc.vector.scalar_tensor_tensor(
+            out=w[:], in0=ta[:], scalar=mean_ta[:], in1=p[:], op0=ALU.subtract, op1=ALU.mult
         )
         mean_c = column("mean_c")
         scratch2 = row_tile("scratch2")

@@ -56,16 +56,14 @@ def tile_attend_hvpageoffsets_kernel(
         q_raw = sb.tile([P, PACK, Q], F32, name="q_raw", align_bytes=64)
         dq_raw = sb.tile([P, PACK, Q], F32, name="dq_raw", align_bytes=64)
         g_raw = sb.tile([P, PACK, Q], F32, name="g_raw", tag="g_raw", align_bytes=64)
-        po_raw = sb.tile([P, PACK * U], F32, name="po_raw", align_bytes=64)
+        po_raw = sb.tile([P, PACK, U], F32, name="po_raw", align_bytes=64)
         base_sb = sb.tile([P, I], F32, name="base_sb", align_bytes=64)
         pf_sb = sb.tile([P, 1], F32, name="pf_sb", align_bytes=64)
-        po_bf = sb.tile([P, (PACK + 1) * U], BF16, name="po_bf", tag="po_bf", align_bytes=64)
 
         nc.vector.memset(k_scales[:, : T // 2].bitcast(I32), 0)
         nc.gpsimd.memset(k_scales[:, T // 2 :].bitcast(I32), 0)
         nc.vector.memset(v_scales[:, : T // 2].bitcast(I32), 0)
         nc.gpsimd.memset(v_scales[:, T // 2 :].bitcast(I32), 0)
-        nc.vector.memset(po_bf[:, PACK * U :], 0.0)
         nc.sync.dma_start(slots[:], offs)
         nc.sync.dma_start(pages[:], offs2)
         nc.sync.dma_start(out=pf_sb[:], in_=pf)
@@ -73,7 +71,7 @@ def tile_attend_hvpageoffsets_kernel(
         nc.sync.dma_start(out=q_raw[:], in_=query.rearrange("(p j) w -> p j w", j=PACK))
         load_scale_rows(nc.sync, k_scales, keys_scales)
         nc.sync.dma_start(out=dq_raw[:], in_=dquery.rearrange("(p j) w -> p j w", j=PACK))
-        nc.sync.dma_start(out=po_raw[:], in_=pofs.rearrange("(p j) w -> p (j w)", j=PACK))
+        nc.sync.dma_start(out=po_raw[:], in_=pofs.rearrange("(p j) w -> p j w", j=PACK))
         nc.sync.dma_start(out=v_words[:].bitcast(I32), in_=vals_words[0].bitcast(I32))
         load_scale_rows(nc.sync, v_scales, vals_scales)
         nc.sync.dma_start(out=g_raw[:], in_=gout.rearrange("(p j) w -> p j w", j=PACK))
@@ -131,13 +129,15 @@ def tile_attend_hvpageoffsets_kernel(
         vs_g = sb.tile([P, I], U8, name="vs_g", tag="neg_a", align_bytes=64)
         nc.vector.tensor_copy(vs_g[:], v_scales[:].indirect(slots[:]))
 
-        nc.scalar.activation(out=po_bf[:, : PACK * U], in_=po_raw[:], func=ACT.Copy)
-        po_grouped = sb.tile([P, G, PACK], BF16, name="po_grouped", tag="po_grouped", align_bytes=64)
+        po_picked = sb.tile([P, PACK, G], BF16, name="po_picked", tag="po_picked", align_bytes=64)
+        po_planes = [sb.tile([P, U], BF16, name="po_plane%d" % t, align_bytes=64) for t in range(PACK)]
         for t in range(PACK):
-            nc.scalar.activation(
-                out=po_grouped[:, :, t], in_=po_bf[:, t * U : (t + 2) * U].indirect(pages[:]), func=ACT.Copy
-            )
-        g_grouped = sb.tile([P, Q, PACK], BF16, name="g_grouped", tag="po_bf", align_bytes=64)
+            nc.scalar.activation(out=po_planes[t][:], in_=po_raw[:, t, :], func=ACT.Copy)
+        for t in range(PACK):
+            nc.scalar.activation(out=po_picked[:, t, :], in_=po_planes[t][:].indirect(pages[:]), func=ACT.Copy)
+        po_grouped = sb.tile([P, G, PACK], BF16, name="po_grouped", tag="po_grouped", align_bytes=64)
+        interleave(nc.scalar.copy, po_grouped[:], po_picked[:])
+        g_grouped = sb.tile([P, Q, PACK], BF16, name="g_grouped", tag="po_picked", align_bytes=64)
         interleave(nc.scalar.copy, g_grouped[:], g_raw[:])
         p = sb.tile([P, I], F32, name="p", tag="g_raw", align_bytes=64)
         z = sb.tile([P, 1], F32, name="z", tag="z", align_bytes=64)

@@ -18,22 +18,27 @@ ACT = mybir.ActivationFunctionType
 
 P = 128
 PACK = 4
+LIST_ROWS = 16
+QUADRANT = 32
+SCALE_ROWS = 4
+RUN = 4
 PAGE = I // G
 GAIN = 512.0
+ALIGN = 64
 
 
-def load_scale_rows(queue, tile, scales):
-    for quad in range(4):
-        queue.dma_start(
-            out=tile[32 * quad : 32 * quad + 4, :].bitcast(I32),
-            in_=scales[0, 4 * quad : 4 * quad + 4, :].bitcast(I32),
+def load_scale_rows(nc, tile, scales):
+    for quad in range(P // QUADRANT):
+        nc.sync.dma_start(
+            out=tile[QUADRANT * quad : QUADRANT * quad + SCALE_ROWS, :].bitcast(I32),
+            in_=scales[0, SCALE_ROWS * quad : SCALE_ROWS * (quad + 1), :].bitcast(I32),
         )
 
 
-def interleave(copy, grouped, raw):
-    copy(
-        out=grouped.rearrange("p (c i) t -> p c t i", i=4),
-        in_=raw.rearrange("p t (c i) -> p c t i", i=4),
+def interleave(nc, grouped, raw):
+    nc.scalar.copy(
+        out=grouped.rearrange("p (c i) t -> p c t i", i=RUN),
+        in_=raw.rearrange("p t (c i) -> p c t i", i=RUN),
     )
 
 
@@ -46,55 +51,72 @@ def tile_attend_hvpageoffsets_kernel(
         sb = ctx.enter_context(tc.tile_pool(name="sb", bufs=1))
         ps = ctx.enter_context(tc.psum_pool(name="ps", bufs=1))
 
-        slots = lists.tile([P, I // 16], U16, name="slots")
-        pages = lists.tile([P, G // 16], U16, name="pages")
+        slots = lists.tile([P, I // LIST_ROWS], U16, name="slots")
+        pages = lists.tile([P, G // LIST_ROWS], U16, name="pages")
 
-        k_words = sb.tile([P, T], U16, name="k_words", align_bytes=64)
-        k_scales = sb.tile([P, T], U8, name="k_scales", tag="k_scales", align_bytes=64)
-        v_words = sb.tile([P, T], U16, name="v_words", tag="v_words", align_bytes=64)
-        v_scales = sb.tile([P, T], U8, name="v_scales", tag="v_scales", align_bytes=64)
-        q_raw = sb.tile([P, PACK, Q], F32, name="q_raw", align_bytes=64)
-        dq_raw = sb.tile([P, PACK, Q], F32, name="dq_raw", align_bytes=64)
-        g_raw = sb.tile([P, PACK, Q], F32, name="g_raw", tag="g_raw", align_bytes=64)
-        po_raw = sb.tile([P, PACK, U], F32, name="po_raw", align_bytes=64)
-        base_sb = sb.tile([P, I], F32, name="base_sb", align_bytes=64)
-        pf_sb = sb.tile([P, 1], F32, name="pf_sb", align_bytes=64)
+        k_words = sb.tile([P, T], U16, name="k_words", align_bytes=ALIGN)
+        k_scales = sb.tile([P, T], U8, name="k_scales", align_bytes=ALIGN)
+        v_words = sb.tile([P, T], U16, name="v_words", tag="v_words", align_bytes=ALIGN)
+        v_scales = sb.tile([P, T], U8, name="v_scales", tag="v_scales", align_bytes=ALIGN)
+        q_raw = sb.tile([P, PACK, Q], F32, name="q_raw", align_bytes=ALIGN)
+        dq_raw = sb.tile([P, PACK, Q], F32, name="dq_raw", align_bytes=ALIGN)
+        g_raw = sb.tile([P, PACK, Q], F32, name="g_raw", tag="g_raw", align_bytes=ALIGN)
+        po_raw = sb.tile([P, PACK * U], F32, name="po_raw", align_bytes=ALIGN)
+        base_sb = sb.tile([P, I], F32, name="base_sb", align_bytes=ALIGN)
+        pf_sb = sb.tile([P, 1], F32, name="pf_sb", align_bytes=ALIGN)
+        po_bf = sb.tile([P, (PACK + 1) * U], BF16, name="po_bf", tag="po_bf", align_bytes=ALIGN)
 
         nc.vector.memset(k_scales[:, : T // 2].bitcast(I32), 0)
         nc.gpsimd.memset(k_scales[:, T // 2 :].bitcast(I32), 0)
         nc.vector.memset(v_scales[:, : T // 2].bitcast(I32), 0)
         nc.gpsimd.memset(v_scales[:, T // 2 :].bitcast(I32), 0)
+        nc.gpsimd.memset(po_bf[:, PACK * U :], 0.0)
+
         nc.sync.dma_start(slots[:], offs)
         nc.sync.dma_start(pages[:], offs2)
         nc.sync.dma_start(out=pf_sb[:], in_=pf)
         nc.sync.dma_start(out=k_words[:].bitcast(I32), in_=keys_words[0].bitcast(I32))
-        nc.sync.dma_start(out=q_raw[:], in_=query.rearrange("(p j) w -> p j w", j=PACK))
-        load_scale_rows(nc.sync, k_scales, keys_scales)
-        nc.sync.dma_start(out=dq_raw[:], in_=dquery.rearrange("(p j) w -> p j w", j=PACK))
-        nc.sync.dma_start(out=po_raw[:], in_=pofs.rearrange("(p j) w -> p j w", j=PACK))
+        nc.sync.dma_start(out=q_raw[:], in_=query.rearrange("(p t) w -> p t w", t=PACK))
+        load_scale_rows(nc, k_scales, keys_scales)
+        nc.sync.dma_start(out=dq_raw[:], in_=dquery.rearrange("(p t) w -> p t w", t=PACK))
+        nc.sync.dma_start(out=po_raw[:], in_=pofs.rearrange("(p t) w -> p (t w)", t=PACK))
         nc.sync.dma_start(out=v_words[:].bitcast(I32), in_=vals_words[0].bitcast(I32))
-        load_scale_rows(nc.sync, v_scales, vals_scales)
-        nc.sync.dma_start(out=g_raw[:], in_=gout.rearrange("(p j) w -> p j w", j=PACK))
+        load_scale_rows(nc, v_scales, vals_scales)
+        nc.sync.dma_start(out=g_raw[:], in_=gout.rearrange("(p t) w -> p t w", t=PACK))
         nc.sync.dma_start(out=base_sb[:], in_=base)
 
-        def quantised():
-            return None
+        def mx_tiles(name, width, grouped_tag):
+            grouped = sb.tile([P, width, PACK], BF16, name=name + "_grouped", tag=grouped_tag, align_bytes=ALIGN)
+            codes = sb.tile([P, width], U32, name=name + "_codes", align_bytes=ALIGN)
+            scales = sb.tile([P, width], U8, name=name + "_scales", align_bytes=ALIGN)
+            return {"grouped": grouped, "codes": codes, "scales": scales}
 
-        def quantise(codes, scales, grouped):
+        def quantise(mx):
             nc.vector.quantize_mx(
-                out=codes.bitcast(FP8X4), scales=scales, in_=grouped.rearrange("p w t -> p (w t)")
+                out=mx["codes"][:].bitcast(FP8X4),
+                scales=mx["scales"][:],
+                in_=mx["grouped"][:].rearrange("p w t -> p (w t)"),
             )
 
-        def product(acc, row_codes, row_scales, moving, moving_scales):
+        def product(acc, rows, moving, moving_scales):
             nc.tensor.matmul_mx(
                 out=acc[:],
-                lhsT=row_codes.bitcast(FP8X4),
-                lhsT_scale=row_scales,
+                lhsT=rows["codes"][:].bitcast(FP8X4),
+                lhsT_scale=rows["scales"][:],
                 rhs=moving,
                 rhs_scale=moving_scales,
                 start=True,
                 stop=True,
             )
+
+        q_mx = mx_tiles("q", Q, "q_grouped")
+        dq_mx = mx_tiles("dq", Q, "dq_grouped")
+        po_mx = mx_tiles("po", G, "po_grouped")
+
+        kw_g = sb.tile([P, I], U16, name="kw_g", align_bytes=ALIGN)
+        ks_g = sb.tile([P, I], U8, name="ks_g", align_bytes=ALIGN)
+        vw_g = sb.tile([P, I], U16, name="vw_g", align_bytes=ALIGN)
+        vs_g = sb.tile([P, I], U8, name="vs_g", align_bytes=ALIGN)
 
         a = ps.tile([P, I], F32, name="a")
         ta = ps.tile([P, I], F32, name="ta")
@@ -102,103 +124,85 @@ def tile_attend_hvpageoffsets_kernel(
         c1 = ps.tile([P, G], F32, name="c1")
 
         def column(name):
-            return sb.tile([P, 1], F32, name=name, align_bytes=64)
+            return sb.tile([P, 1], F32, name=name, align_bytes=ALIGN)
 
         def row_tile(name):
-            return sb.tile([P, I], F32, name=name, align_bytes=64)
+            return sb.tile([P, I], F32, name=name, align_bytes=ALIGN)
 
-        qd_grouped = sb.tile([P, 2 * Q, PACK], BF16, name="qd_grouped", tag="qd_grouped", align_bytes=64)
-        interleave(nc.scalar.copy, qd_grouped[:, :Q, :], q_raw[:])
-        interleave(nc.scalar.copy, qd_grouped[:, Q:, :], dq_raw[:])
-        kw_g = sb.tile([P, I], U16, name="kw_g", align_bytes=64)
-        nc.vector.tensor_copy(kw_g[:], k_words[:].indirect(slots[:]))
-        ks_g = sb.tile([P, I], U8, name="ks_g", align_bytes=64)
+        interleave(nc, q_mx["grouped"][:], q_raw[:])
+        interleave(nc, dq_mx["grouped"][:], dq_raw[:])
         nc.vector.tensor_copy(ks_g[:], k_scales[:].indirect(slots[:]))
-        qd_codes = sb.tile([P, 2 * Q], U32, name="qd_codes", tag="k_scales", align_bytes=64)
-        qd_scales = sb.tile([P, 2 * Q], U8, name="qd_scales", align_bytes=64)
-        quantise(qd_codes[:], qd_scales[:], qd_grouped[:])
-        product(a, qd_codes[:, :Q], qd_scales[:, :Q], kw_g[:].bitcast(FP4X4), ks_g[:])
-        product(ta, qd_codes[:, Q:], qd_scales[:, Q:], kw_g[:].bitcast(FP4X4), ks_g[:])
-        vw_g = sb.tile([P, I], U16, name="vw_g", tag="qd_grouped", align_bytes=64)
-        nc.vector.tensor_copy(vw_g[:], v_words[:].indirect(slots[:]))
-        neg_max = sb.tile([P, 1], F32, name="neg_max", tag="v_words", align_bytes=64)
-        neg_a = sb.tile([P, I], F32, name="neg_a", tag="neg_a", align_bytes=64)
-        nc.vector.tensor_scalar(
-            out=neg_a[:], in0=a[:], scalar1=-1.0, scalar2=None, op0=ALU.mult, op1=ALU.min, accum_out=neg_max[:]
-        )
-        vs_g = sb.tile([P, I], U8, name="vs_g", tag="neg_a", align_bytes=64)
-        nc.vector.tensor_copy(vs_g[:], v_scales[:].indirect(slots[:]))
+        quantise(q_mx)
+        nc.vector.tensor_copy(kw_g[:], k_words[:].indirect(slots[:]))
+        product(a, q_mx, kw_g[:].bitcast(FP4X4), ks_g[:])
+        quantise(dq_mx)
+        product(ta, dq_mx, kw_g[:].bitcast(FP4X4), ks_g[:])
 
-        po_picked = sb.tile([P, PACK, G], BF16, name="po_picked", tag="po_picked", align_bytes=64)
-        po_planes = [sb.tile([P, U], BF16, name="po_plane%d" % t, align_bytes=64) for t in range(PACK)]
+        nc.scalar.activation(out=po_bf[:, : PACK * U], in_=po_raw[:], func=ACT.Copy)
         for t in range(PACK):
-            nc.scalar.activation(out=po_planes[t][:], in_=po_raw[:, t, :], func=ACT.Copy)
-        for t in range(PACK):
-            nc.scalar.activation(out=po_picked[:, t, :], in_=po_planes[t][:].indirect(pages[:]), func=ACT.Copy)
-        po_grouped = sb.tile([P, G, PACK], BF16, name="po_grouped", tag="po_grouped", align_bytes=64)
-        interleave(nc.scalar.copy, po_grouped[:], po_picked[:])
-        g_grouped = sb.tile([P, Q, PACK], BF16, name="g_grouped", tag="po_picked", align_bytes=64)
-        interleave(nc.scalar.copy, g_grouped[:], g_raw[:])
-        p = sb.tile([P, I], F32, name="p", tag="g_raw", align_bytes=64)
-        z = sb.tile([P, 1], F32, name="z", tag="z", align_bytes=64)
+            nc.scalar.activation(
+                out=po_mx["grouped"][:, :, t], in_=po_bf[:, t * U : (t + 2) * U].indirect(pages[:]), func=ACT.Copy
+            )
+
+        neg_max = sb.tile([P, 1], F32, name="neg_max", tag="after_exp", align_bytes=ALIGN)
+        nc.vector.tensor_reduce(out=neg_max[:], in_=a[:], axis=mybir.AxisListType.X, op=ALU.max, negate=True)
+        p = sb.tile([P, I], F32, name="p", tag="po_bf", align_bytes=ALIGN)
+        z = column("z")
         nc.scalar.activation(out=p[:], in_=a[:], func=ACT.Exp, bias=neg_max[:], accum_out=z[:])
 
-        rz = sb.tile([P, 1], F32, name="rz", tag="v_scales", align_bytes=64)
+        g_mx = mx_tiles("g", Q, "after_exp")
+        interleave(nc, g_mx["grouped"][:], g_raw[:])
+        nc.vector.tensor_copy(vw_g[:], v_words[:].indirect(slots[:]))
+        nc.vector.tensor_copy(vs_g[:], v_scales[:].indirect(slots[:]))
+        quantise(po_mx)
+        quantise(g_mx)
+        product(c0, g_mx, vw_g[:].bitcast(FP4X4), vs_g[:])
+        product(c1, g_mx, po_mx["codes"][:].bitcast(FP8X4), po_mx["scales"][:])
+
+        rz = sb.tile([P, 1], F32, name="rz", tag="after_exp", align_bytes=ALIGN)
         nc.vector.reciprocal(out=rz[:], in_=z[:])
-        gp_codes = sb.tile([P, Q + G], U32, name="gp_codes", tag="z", align_bytes=64)
-        g_scales = sb.tile([P, Q], U8, name="g_scales", align_bytes=64)
-        po_scales = sb.tile([P, G], U8, name="po_scales", align_bytes=64)
-        quantise(gp_codes[:, :Q], g_scales[:], g_grouped[:])
-        product(c0, gp_codes[:, :Q], g_scales[:], vw_g[:].bitcast(FP4X4), vs_g[:])
-        quantise(gp_codes[:, Q:], po_scales[:], po_grouped[:])
-        product(c1, gp_codes[:, :Q], g_scales[:], gp_codes[:, Q:].bitcast(FP8X4), po_scales[:])
+        pn = sb.tile([P, I], F32, name="pn", tag="g_raw", align_bytes=ALIGN)
+        nc.scalar.activation(out=pn[:], in_=p[:], func=ACT.Copy, scale=rz[:])
+        neg_pf = column("neg_pf")
+        nc.gpsimd.tensor_scalar(out=neg_pf[:], in0=pf_sb[:], scalar1=-GAIN, scalar2=0.0, op0=ALU.mult, op1=ALU.add)
+        page_term = sb.tile([P, G], F32, name="page_term", align_bytes=ALIGN)
+        nc.scalar.activation(out=page_term[:], in_=c1[:], func=ACT.Copy, scale=neg_pf[:])
 
-        scratch = sb.tile([P, I], F32, name="scratch", tag="po_grouped", align_bytes=64)
-        mean_ta = column("mean_ta")
+        cn = row_tile("cn")
         nc.vector.scalar_tensor_tensor(
-            out=scratch[:], in0=ta[:], scalar=rz[:], in1=p[:], op0=ALU.mult, op1=ALU.mult, accum_out=mean_ta[:]
-        )
-        gain_pf = column("gain_pf")
-        nc.gpsimd.tensor_scalar(out=gain_pf[:], in0=pf_sb[:], scalar1=GAIN, scalar2=0.0, op0=ALU.mult, op1=ALU.add)
-        neg_rz2 = column("neg_rz2")
-        nc.gpsimd.tensor_scalar(out=neg_rz2[:], in0=rz[:], scalar1=rz[:], scalar2=-1.0, op0=ALU.mult, op1=ALU.mult)
-        page_term = sb.tile([P, G], F32, name="page_term", tag="page_term", align_bytes=64)
-        nc.scalar.activation(out=page_term[:], in_=c1[:], func=ACT.Copy, scale=gain_pf[:])
-
-        c = row_tile("c")
-        nc.vector.scalar_tensor_tensor(
-            out=c[:].rearrange("p (g j) -> p g j", j=PAGE),
+            out=cn[:].rearrange("p (g j) -> p g j", j=PAGE),
             in0=c0[:].rearrange("p (g j) -> p g j", j=PAGE),
-            scalar=GAIN,
+            scalar=-GAIN,
             in1=page_term[:].unsqueeze(2).to_broadcast([P, G, PAGE]),
             op0=ALU.mult,
             op1=ALU.add,
         )
-        w = sb.tile([P, I], F32, name="w", tag="page_term", align_bytes=64)
+        ta_terms = sb.tile([P, I], F32, name="ta_terms", tag="v_scales", align_bytes=ALIGN)
+        mean_ta = sb.tile([P, 1], F32, name="mean_ta", tag="v_words", align_bytes=ALIGN)
         nc.vector.scalar_tensor_tensor(
-            out=w[:], in0=ta[:], scalar=mean_ta[:], in1=p[:], op0=ALU.subtract, op1=ALU.mult
+            out=ta_terms[:], in0=ta[:], scalar=rz[:], in1=p[:], op0=ALU.mult, op1=ALU.mult, accum_out=mean_ta[:]
         )
-        mean_c = column("mean_c")
-        scratch2 = row_tile("scratch2")
+        mean_cn = column("mean_cn")
+        cn_terms = row_tile("cn_terms")
         nc.vector.scalar_tensor_tensor(
-            out=scratch2[:], in0=c[:], scalar=rz[:], in1=p[:], op0=ALU.mult, op1=ALU.mult, accum_out=mean_c[:]
+            out=cn_terms[:], in0=cn[:], scalar=rz[:], in1=p[:], op0=ALU.mult, op1=ALU.mult, accum_out=mean_cn[:]
         )
-        y = row_tile("y")
-        cov_z = column("cov_z")
+        w = row_tile("w")
         nc.vector.scalar_tensor_tensor(
-            out=y[:], in0=c[:], scalar=mean_c[:], in1=w[:], op0=ALU.subtract, op1=ALU.mult, accum_out=cov_z[:]
+            out=w[:], in0=ta[:], scalar=mean_ta[:], in1=pn[:], op0=ALU.subtract, op1=ALU.mult
         )
-        p_factor = column("p_factor")
-        nc.scalar.activation(out=p_factor[:], in_=cov_z[:], func=ACT.Copy, scale=neg_rz2[:])
+        yn = row_tile("yn")
+        neg_cov = column("neg_cov")
+        nc.vector.scalar_tensor_tensor(
+            out=yn[:], in0=cn[:], scalar=mean_cn[:], in1=w[:], op0=ALU.subtract, op1=ALU.mult, accum_out=neg_cov[:]
+        )
         halves = [slice(0, I // 2), slice(I // 2, I)]
-        y1 = row_tile("y1")
+        partial = row_tile("partial")
         res = row_tile("res")
         for h in halves:
-            nc.vector.scalar_tensor_tensor(
-                out=y1[:, h], in0=y[:, h], scalar=rz[:], in1=base_sb[:, h], op0=ALU.mult, op1=ALU.add
-            )
+            nc.vector.tensor_tensor(out=partial[:, h], in0=base_sb[:, h], in1=yn[:, h], op=ALU.subtract)
         for h in halves:
             nc.vector.scalar_tensor_tensor(
-                out=res[:, h], in0=p[:, h], scalar=p_factor[:], in1=y1[:, h], op0=ALU.mult, op1=ALU.add
+                out=res[:, h], in0=pn[:, h], scalar=neg_cov[:], in1=partial[:, h], op0=ALU.mult, op1=ALU.add
             )
             nc.sync.dma_start(out=out[:, h], in_=res[:, h])

from contextlib import ExitStack

import concourse.mybir as mybir

D, E, T, I, Q, G, U = 512, 512, 2048, 512, 128, 64, 256
FLOPS = 2 * Q * (2 * D * I + E * I + E * G)

F32 = mybir.dt.float32
BF16 = mybir.dt.bfloat16
I32 = mybir.dt.int32
U32 = mybir.dt.uint32
U16 = mybir.dt.uint16
U8 = mybir.dt.uint8
FP8X4 = mybir.dt.float8_e4m3fn_x4
FP4X4 = mybir.dt.float4_e2m1fn_x4
ALU = mybir.AluOpType
ACT = mybir.ActivationFunctionType

P = 128
PACK = 4
LIST_ROWS = 16
QUADRANT = 32
SCALE_ROWS = 4
RUN = 4
PAGE = I // G
GAIN = 512.0
ALIGN = 64


def load_scale_rows(nc, tile, scales):
    for quad in range(P // QUADRANT):
        nc.sync.dma_start(
            out=tile[QUADRANT * quad : QUADRANT * quad + SCALE_ROWS, :].bitcast(I32),
            in_=scales[0, SCALE_ROWS * quad : SCALE_ROWS * (quad + 1), :].bitcast(I32),
        )


def interleave(nc, grouped, raw):
    nc.scalar.copy(
        out=grouped.rearrange("p (c i) t -> p c t i", i=RUN),
        in_=raw.rearrange("p t (c i) -> p c t i", i=RUN),
    )


def tile_attend_hvpageoffsets_kernel(
    tc, query, keys_words, keys_scales, gout, vals_words, vals_scales, pofs, pf, dquery, base, offs, offs2, out
):
    nc = tc.nc
    with ExitStack() as ctx:
        lists = ctx.enter_context(tc.tile_pool(name="lists", bufs=1))
        sb = ctx.enter_context(tc.tile_pool(name="sb", bufs=1))
        ps = ctx.enter_context(tc.psum_pool(name="ps", bufs=1))

        slots = lists.tile([P, I // LIST_ROWS], U16, name="slots")
        pages = lists.tile([P, G // LIST_ROWS], U16, name="pages")

        k_words = sb.tile([P, T], U16, name="k_words", align_bytes=ALIGN)
        k_scales = sb.tile([P, T], U8, name="k_scales", align_bytes=ALIGN)
        v_words = sb.tile([P, T], U16, name="v_words", tag="v_words", align_bytes=ALIGN)
        v_scales = sb.tile([P, T], U8, name="v_scales", tag="v_scales", align_bytes=ALIGN)
        q_raw = sb.tile([P, PACK, Q], F32, name="q_raw", align_bytes=ALIGN)
        dq_raw = sb.tile([P, PACK, Q], F32, name="dq_raw", align_bytes=ALIGN)
        g_raw = sb.tile([P, PACK, Q], F32, name="g_raw", tag="g_raw", align_bytes=ALIGN)
        po_raw = sb.tile([P, PACK * U], F32, name="po_raw", align_bytes=ALIGN)
        base_sb = sb.tile([P, I], F32, name="base_sb", align_bytes=ALIGN)
        pf_sb = sb.tile([P, 1], F32, name="pf_sb", align_bytes=ALIGN)
        po_bf = sb.tile([P, (PACK + 1) * U], BF16, name="po_bf", tag="po_bf", align_bytes=ALIGN)

        nc.vector.memset(k_scales[:, : T // 2].bitcast(I32), 0)
        nc.gpsimd.memset(k_scales[:, T // 2 :].bitcast(I32), 0)
        nc.vector.memset(v_scales[:, : T // 2].bitcast(I32), 0)
        nc.gpsimd.memset(v_scales[:, T // 2 :].bitcast(I32), 0)
        nc.gpsimd.memset(po_bf[:, PACK * U :], 0.0)

        nc.sync.dma_start(slots[:], offs)
        nc.sync.dma_start(pages[:], offs2)
        nc.sync.dma_start(out=pf_sb[:], in_=pf)
        nc.sync.dma_start(out=k_words[:].bitcast(I32), in_=keys_words[0].bitcast(I32))
        nc.sync.dma_start(out=q_raw[:], in_=query.rearrange("(p t) w -> p t w", t=PACK))
        load_scale_rows(nc, k_scales, keys_scales)
        nc.sync.dma_start(out=dq_raw[:], in_=dquery.rearrange("(p t) w -> p t w", t=PACK))
        nc.sync.dma_start(out=po_raw[:], in_=pofs.rearrange("(p t) w -> p (t w)", t=PACK))
        nc.sync.dma_start(out=v_words[:].bitcast(I32), in_=vals_words[0].bitcast(I32))
        load_scale_rows(nc, v_scales, vals_scales)
        nc.sync.dma_start(out=g_raw[:], in_=gout.rearrange("(p t) w -> p t w", t=PACK))
        nc.sync.dma_start(out=base_sb[:], in_=base)

        def mx_tiles(name, width, grouped_tag):
            grouped = sb.tile([P, width, PACK], BF16, name=name + "_grouped", tag=grouped_tag, align_bytes=ALIGN)
            codes = sb.tile([P, width], U32, name=name + "_codes", align_bytes=ALIGN)
            scales = sb.tile([P, width], U8, name=name + "_scales", align_bytes=ALIGN)
            return {"grouped": grouped, "codes": codes, "scales": scales}

        def quantise(mx):
            nc.vector.quantize_mx(
                out=mx["codes"][:].bitcast(FP8X4),
                scales=mx["scales"][:],
                in_=mx["grouped"][:].rearrange("p w t -> p (w t)"),
            )

        def product(acc, rows, moving, moving_scales):
            nc.tensor.matmul_mx(
                out=acc[:],
                lhsT=rows["codes"][:].bitcast(FP8X4),
                lhsT_scale=rows["scales"][:],
                rhs=moving,
                rhs_scale=moving_scales,
                start=True,
                stop=True,
            )

        q_mx = mx_tiles("q", Q, "q_grouped")
        dq_mx = mx_tiles("dq", Q, "dq_grouped")
        po_mx = mx_tiles("po", G, "po_grouped")

        kw_g = sb.tile([P, I], U16, name="kw_g", align_bytes=ALIGN)
        ks_g = sb.tile([P, I], U8, name="ks_g", align_bytes=ALIGN)
        vw_g = sb.tile([P, I], U16, name="vw_g", align_bytes=ALIGN)
        vs_g = sb.tile([P, I], U8, name="vs_g", align_bytes=ALIGN)

        a = ps.tile([P, I], F32, name="a")
        ta = ps.tile([P, I], F32, name="ta")
        c0 = ps.tile([P, I], F32, name="c0")
        c1 = ps.tile([P, G], F32, name="c1")

        def column(name):
            return sb.tile([P, 1], F32, name=name, align_bytes=ALIGN)

        def row_tile(name):
            return sb.tile([P, I], F32, name=name, align_bytes=ALIGN)

        interleave(nc, q_mx["grouped"][:], q_raw[:])
        interleave(nc, dq_mx["grouped"][:], dq_raw[:])
        nc.vector.tensor_copy(ks_g[:], k_scales[:].indirect(slots[:]))
        quantise(q_mx)
        nc.vector.tensor_copy(kw_g[:], k_words[:].indirect(slots[:]))
        product(a, q_mx, kw_g[:].bitcast(FP4X4), ks_g[:])
        quantise(dq_mx)
        product(ta, dq_mx, kw_g[:].bitcast(FP4X4), ks_g[:])

        nc.scalar.activation(out=po_bf[:, : PACK * U], in_=po_raw[:], func=ACT.Copy)
        for t in range(PACK):
            nc.scalar.activation(
                out=po_mx["grouped"][:, :, t], in_=po_bf[:, t * U : (t + 2) * U].indirect(pages[:]), func=ACT.Copy
            )

        neg_max = sb.tile([P, 1], F32, name="neg_max", tag="after_exp", align_bytes=ALIGN)
        nc.vector.tensor_reduce(out=neg_max[:], in_=a[:], axis=mybir.AxisListType.X, op=ALU.max, negate=True)
        p = sb.tile([P, I], F32, name="p", tag="po_bf", align_bytes=ALIGN)
        z = column("z")
        nc.scalar.activation(out=p[:], in_=a[:], func=ACT.Exp, bias=neg_max[:], accum_out=z[:])

        g_mx = mx_tiles("g", Q, "after_exp")
        interleave(nc, g_mx["grouped"][:], g_raw[:])
        nc.vector.tensor_copy(vw_g[:], v_words[:].indirect(slots[:]))
        nc.vector.tensor_copy(vs_g[:], v_scales[:].indirect(slots[:]))
        quantise(po_mx)
        quantise(g_mx)
        product(c0, g_mx, vw_g[:].bitcast(FP4X4), vs_g[:])
        product(c1, g_mx, po_mx["codes"][:].bitcast(FP8X4), po_mx["scales"][:])

        rz = sb.tile([P, 1], F32, name="rz", tag="after_exp", align_bytes=ALIGN)
        nc.vector.reciprocal(out=rz[:], in_=z[:])
        pn = sb.tile([P, I], F32, name="pn", tag="g_raw", align_bytes=ALIGN)
        nc.scalar.activation(out=pn[:], in_=p[:], func=ACT.Copy, scale=rz[:])
        neg_pf = column("neg_pf")
        nc.gpsimd.tensor_scalar(out=neg_pf[:], in0=pf_sb[:], scalar1=-GAIN, scalar2=0.0, op0=ALU.mult, op1=ALU.add)
        page_term = sb.tile([P, G], F32, name="page_term", align_bytes=ALIGN)
        nc.scalar.activation(out=page_term[:], in_=c1[:], func=ACT.Copy, scale=neg_pf[:])

        cn = row_tile("cn")
        nc.vector.scalar_tensor_tensor(
            out=cn[:].rearrange("p (g j) -> p g j", j=PAGE),
            in0=c0[:].rearrange("p (g j) -> p g j", j=PAGE),
            scalar=-GAIN,
            in1=page_term[:].unsqueeze(2).to_broadcast([P, G, PAGE]),
            op0=ALU.mult,
            op1=ALU.add,
        )
        ta_terms = sb.tile([P, I], F32, name="ta_terms", tag="v_scales", align_bytes=ALIGN)
        mean_ta = sb.tile([P, 1], F32, name="mean_ta", tag="v_words", align_bytes=ALIGN)
        nc.vector.scalar_tensor_tensor(
            out=ta_terms[:], in0=ta[:], scalar=rz[:], in1=p[:], op0=ALU.mult, op1=ALU.mult, accum_out=mean_ta[:]
        )
        mean_cn = column("mean_cn")
        cn_terms = row_tile("cn_terms")
        nc.vector.scalar_tensor_tensor(
            out=cn_terms[:], in0=cn[:], scalar=rz[:], in1=p[:], op0=ALU.mult, op1=ALU.mult, accum_out=mean_cn[:]
        )
        w = row_tile("w")
        nc.vector.scalar_tensor_tensor(
            out=w[:], in0=ta[:], scalar=mean_ta[:], in1=pn[:], op0=ALU.subtract, op1=ALU.mult
        )
        yn = row_tile("yn")
        neg_cov = column("neg_cov")
        nc.vector.scalar_tensor_tensor(
            out=yn[:], in0=cn[:], scalar=mean_cn[:], in1=w[:], op0=ALU.subtract, op1=ALU.mult, accum_out=neg_cov[:]
        )
        halves = [slice(0, I // 2), slice(I // 2, I)]
        partial = row_tile("partial")
        res = row_tile("res")
        for h in halves:
            nc.vector.tensor_tensor(out=partial[:, h], in0=base_sb[:, h], in1=yn[:, h], op=ALU.subtract)
        for h in halves:
            nc.vector.scalar_tensor_tensor(
                out=res[:, h], in0=pn[:, h], scalar=neg_cov[:], in1=partial[:, h], op0=ALU.mult, op1=ALU.add
            )
            nc.sync.dma_start(out=out[:, h], in_=res[:, h])
